import numpy as np
import ml_dtypes


def mxq(x, axis, fmt="e4m3"):
    dtype, down = {"e4m3": (ml_dtypes.float8_e4m3fn, 7), "e5m2": (ml_dtypes.float8_e5m2, 14)}[fmt]
    v = np.moveaxis(np.asarray(x, np.float32).astype(ml_dtypes.bfloat16).astype(np.float64), axis, -1)
    blocks = v.reshape(v.shape[:-1] + (-1, 32))
    amax = np.abs(blocks).max(-1, keepdims=True)
    byte = np.maximum(np.where(amax > 0, np.frexp(amax)[1] - 1 + 127, 0) - down, 1)
    scale = np.exp2(byte - 127.0)
    codes = (blocks / scale).astype(np.float32).astype(dtype).astype(np.float64)
    return np.moveaxis((codes * scale).reshape(v.shape), -1, axis)


WIDE = False


def mx_kscale(k):
    if not WIDE:
        return np.ones(k)
    levels = np.array([10, -10, 5, -5, 0])
    if k % 512:
        return np.exp2(np.random.permutation(np.resize(levels, k // 32))).repeat(32)
    a = np.empty((k // 512, 16))
    for p in range(k // 512):
        a[p, :8] = np.random.permutation(np.resize(levels, 8))
        for g in range(8):
            far = levels[np.abs(levels - a[p, g]) >= 10]
            a[p, g + 8] = far[np.random.randint(len(far))]
    return np.exp2(a.ravel()).repeat(32)


def f64(x):
    return np.asarray(x).astype(np.float64)


def striped8(idx):
    return np.concatenate([v.reshape(-1, 16).T for v in idx]).astype(np.uint16)


def unstriped8(offs):
    return np.stack([offs[16 * g:16 * g + 16].T.reshape(-1) for g in range(8)]).astype(np.int64)


def split(x):
    m, e = np.frexp(f64(x))
    hi = np.ldexp(np.trunc(16.0 * m) / 16.0, e)
    return hi, f64(x) - hi


K, M, T, S = 512, 256, 1024, 512


def setup_inputs():
    n = np.random.standard_normal
    s = mx_kscale(K)[:, None]
    return {
        "xT": (n((K, T)) * s).astype(np.float32),
        "w": (n((K, M)) / np.sqrt(K) / s).astype(np.float32),
        "wgt": np.repeat(np.random.uniform(0.5, 2.0, (8, S)), 16, axis=0).astype(np.float32),
        "offs": striped8(np.stack([np.random.permutation(T)[:S] for _ in range(8)])),
    }


def reference(xT, w, wgt, offs):
    idx = unstriped8(offs)
    group = np.arange(K) % 512 // 64
    xg = f64(wgt)[np.arange(K) // 4 % 128] * f64(xT)[np.arange(K)[:, None], idx[group]]
    xT_ = mxq(xg, 0, "e4m3")
    w_hi, w_lo = split(w)
    w_hi_, w_lo_ = mxq(w_hi, 0, "e4m3"), mxq(w_lo, 0, "e4m3")
    y = w_hi_.T @ xT_ + w_lo_.T @ xT_
    return y

@@ -1,0 +1,130 @@
+from contextlib import ExitStack
+
+import concourse.mybir as mybir
+
+F32 = mybir.dt.float32
+BF16 = mybir.dt.bfloat16
+I32 = mybir.dt.int32
+U32 = mybir.dt.uint32
+U16 = mybir.dt.uint16
+U8 = mybir.dt.uint8
+FP8X4 = mybir.dt.float8_e4m3fn_x4
+ALU = mybir.AluOpType
+
+P, J = 128, 4
+K, M, T, S = 512, 256, 1024, 512
+FLOPS = 2 * 2 * K * M * S
+MASK = -(1 << 20)
+
+
+def tile_list_heads_hl_none_kernel(tc, xT, w, wgt, offs, out):
+    nc = tc.nc
+    with ExitStack() as ctx:
+        keep = ctx.enter_context(tc.tile_pool(name="keep", bufs=1))
+        psum = ctx.enter_context(tc.psum_pool(name="psum", bufs=1))
+
+        w_raw = keep.tile([P, J, M], F32, name="w_raw", align_bytes=64)
+        lists = keep.tile([P, S // 16], U16, name="lists")
+        weights = keep.tile([P, S], F32, name="weights", align_bytes=64)
+        w_view = w.rearrange("(p j) n -> p j n", j=J)
+        nc.sync.dma_start(w_raw[:, 0:2, :], w_view[:, 0:2, :])
+        nc.sync.dma_start(w_raw[:, 2:4, :], w_view[:, 2:4, :])
+        nc.sync.dma_start(lists[:], offs)
+        nc.sync.dma_start(weights[:], wgt)
+        x_view = xT.rearrange("(p j) t -> p j t", j=J)
+        planes = []
+        for j in range(J):
+            plane = keep.tile([P, T], F32, name=f"plane{j}", align_bytes=64)
+            nc.sync.dma_start(plane[:], x_view[:, j, :])
+            planes.append(plane)
+
+        w_hi = keep.tile([P, J, M], I32, name="w_hi", align_bytes=64)
+        w_bf = keep.tile([P, 2 * M, J], BF16, name="w_bf", align_bytes=64)
+        for h in range(2):
+            js = slice(2 * h, 2 * h + 2)
+            nc.vector.tensor_scalar(w_hi[:, js, :], w_raw[:, js, :].bitcast(I32), MASK, None, ALU.bitwise_and)
+        nc.scalar.copy(w_bf[:, 0:M, :], w_hi[:].bitcast(F32).rearrange("p j n -> p n j"))
+        nc.vector.tensor_tensor(
+            w_bf[:, M : 2 * M, :],
+            w_raw[:].rearrange("p j n -> p n j"),
+            w_hi[:].bitcast(F32).rearrange("p j n -> p n j"),
+            ALU.subtract,
+        )
+
+        def quantize(src, width, name):
+            codes = keep.tile([P, width], U32, name=f"{name}_codes", align_bytes=64)
+            scales = keep.tile([P, width], U8, name=f"{name}_scales", align_bytes=64)
+            nc.vector.quantize_mx(
+                out=codes[:].bitcast(FP8X4), scales=scales[:], in_=src.rearrange("p n j -> p (n j)")
+            )
+            return codes, scales
+
+        picked = keep.tile([P, 7, 256], F32, name="picked", align_bytes=64)
+        rows = ((0, 1, 2, 3), (5, 6, 3, 4))
+        xg = [keep.tile([P, 256, J], BF16, name=f"xg{h}", align_bytes=64) for h in range(2)]
+
+        def gather(j, start, width):
+            half, c = start // 256, start % 256
+            nc.vector.tensor_tensor(
+                picked[:, rows[half][j], c : c + width],
+                planes[j][:].indirect(lists[:, start // 16 : (start + width) // 16]),
+                weights[:, start : start + width],
+                ALU.mult,
+            )
+
+        def interleave(pair, start, width):
+            half, c = start // 256, start % 256
+            r = rows[half][2 * pair]
+            nc.scalar.copy(
+                xg[half][:, c : c + width, 2 * pair : 2 * pair + 2],
+                picked[:, r : r + 2, c : c + width].rearrange("p j n -> p n j"),
+            )
+
+        results = []
+
+        def multiply(x, start, width):
+            for m in range(2):
+                acc = psum.tile([P, width], F32, name=f"acc{start}_{m}")
+                codes, scales = w_q
+                for side in range(2):
+                    cols = slice(side * M + m * P, side * M + (m + 1) * P)
+                    nc.tensor.matmul_mx(
+                        out=acc[:],
+                        lhsT=codes[:, cols].bitcast(FP8X4),
+                        lhsT_scale=scales[:, cols],
+                        rhs=x[0][:].bitcast(FP8X4),
+                        rhs_scale=x[1][:],
+                        start=side == 0,
+                        stop=side == 1,
+                    )
+                results.append((acc, m, start, width))
+
+        w_q = quantize(w_bf[:], 2 * M, "w")
+        gather(0, 0, 256)
+        gather(0, 256, 256)
+        gather(1, 0, 256)
+        interleave(0, 0, 256)
+        gather(1, 256, 256)
+        gather(2, 0, 256)
+        gather(3, 0, 256)
+        interleave(1, 0, 256)
+        x_a = quantize(xg[0][:], 256, "xa")
+        multiply(x_a, 0, 256)
+        gather(3, 256, 256)
+        interleave(0, 256, 256)
+        gather(2, 256, 128)
+        interleave(1, 256, 128)
+        gather(2, 384, 128)
+        interleave(1, 384, 128)
+        x_b = quantize(xg[1][:, 0:128, :], 128, "xb")
+        multiply(x_b, 256, 128)
+        x_c = quantize(xg[1][:, 128:256, :], 128, "xc")
+        multiply(x_c, 384, 128)
+
+        for acc, m, start, width in results:
+            res = keep.tile([P, width], F32, name=f"res{start}_{m}", align_bytes=64)
+            if m == 0:
+                nc.scalar.copy(res[:], acc[:])
+            else:
+                nc.vector.tensor_copy(res[:], acc[:])
+            nc.sync.dma_start(out[m * P : (m + 1) * P, start : start + width], res[:])

@@ -25,18 +25,19 @@ def tile_list_heads_hl_none_kernel(tc, xT, w, wgt, offs, out):
 
         w_raw = keep.tile([P, J, M], F32, name="w_raw", align_bytes=64)
         lists = keep.tile([P, S // 16], U16, name="lists")
-        weights = keep.tile([P, S], F32, name="weights", align_bytes=64)
+        weights = [keep.tile([P, n], F32, name=f"weights{n}", align_bytes=64) for n in (384, 128)]
         w_view = w.rearrange("(p j) n -> p j n", j=J)
         nc.sync.dma_start(w_raw[:, 0:2, :], w_view[:, 0:2, :])
         nc.sync.dma_start(w_raw[:, 2:4, :], w_view[:, 2:4, :])
         nc.sync.dma_start(lists[:], offs)
-        nc.sync.dma_start(weights[:], wgt)
+        nc.sync.dma_start(weights[0][:], wgt[:, 0:384])
         x_view = xT.rearrange("(p j) t -> p j t", j=J)
         planes = []
         for j in range(J):
             plane = keep.tile([P, T], F32, name=f"plane{j}", align_bytes=64)
             nc.sync.dma_start(plane[:], x_view[:, j, :])
             planes.append(plane)
+        nc.sync.dma_start(weights[1][:], wgt[:, 384:512])
 
         w_hi = keep.tile([P, J, M], I32, name="w_hi", align_bytes=64)
         w_bf = keep.tile([P, 2 * M, J], BF16, name="w_bf", align_bytes=64)
@@ -59,25 +60,23 @@ def tile_list_heads_hl_none_kernel(tc, xT, w, wgt, offs, out):
             )
             return codes, scales
 
-        picked = keep.tile([P, 7, 256], F32, name="picked", align_bytes=64)
-        rows = ((0, 1, 2, 3), (5, 6, 3, 4))
-        xg = [keep.tile([P, 256, J], BF16, name=f"xg{h}", align_bytes=64) for h in range(2)]
+        picked = keep.tile([P, J, 384], F32, name="picked", align_bytes=64)
+        xg = [keep.tile([P, n, J], BF16, name=f"xg{n}", align_bytes=64) for n in (384, 128)]
 
         def gather(j, start, width):
-            half, c = start // 256, start % 256
+            h, c = start // 384, start % 384
             nc.vector.tensor_tensor(
-                picked[:, rows[half][j], c : c + width],
+                picked[:, j, c : c + width],
                 planes[j][:].indirect(lists[:, start // 16 : (start + width) // 16]),
-                weights[:, start : start + width],
+                weights[h][:, c : c + width],
                 ALU.mult,
             )
 
         def interleave(pair, start, width):
-            half, c = start // 256, start % 256
-            r = rows[half][2 * pair]
+            h, c = start // 384, start % 384
             nc.scalar.copy(
-                xg[half][:, c : c + width, 2 * pair : 2 * pair + 2],
-                picked[:, r : r + 2, c : c + width].rearrange("p j n -> p n j"),
+                xg[h][:, c : c + width, 2 * pair : 2 * pair + 2],
+                picked[:, 2 * pair : 2 * pair + 2, c : c + width].rearrange("p j n -> p n j"),
             )
 
         results = []
@@ -100,30 +99,30 @@ def tile_list_heads_hl_none_kernel(tc, xT, w, wgt, offs, out):
                 results.append((acc, m, start, width))
 
         w_q = quantize(w_bf[:], 2 * M, "w")
-        gather(0, 0, 256)
-        gather(0, 256, 256)
-        gather(1, 0, 256)
-        interleave(0, 0, 256)
-        gather(1, 256, 256)
-        gather(2, 0, 256)
+        gather(0, 0, 384)
+        gather(1, 0, 384)
+        interleave(0, 0, 384)
+        gather(2, 0, 384)
         gather(3, 0, 256)
         interleave(1, 0, 256)
-        x_a = quantize(xg[0][:], 256, "xa")
-        multiply(x_a, 0, 256)
-        gather(3, 256, 256)
-        interleave(0, 256, 256)
-        gather(2, 256, 128)
+        gather(3, 256, 128)
         interleave(1, 256, 128)
+        gather(0, 384, 128)
+        gather(1, 384, 128)
+        x_a = quantize(xg[0][:, 0:256, :], 256, "xa")
+        multiply(x_a, 0, 256)
+        interleave(0, 384, 128)
         gather(2, 384, 128)
+        gather(3, 384, 128)
         interleave(1, 384, 128)
-        x_b = quantize(xg[1][:, 0:128, :], 128, "xb")
+        x_b = quantize(xg[0][:, 256:384, :], 128, "xb")
         multiply(x_b, 256, 128)
-        x_c = quantize(xg[1][:, 128:256, :], 128, "xc")
+        x_c = quantize(xg[1][:], 128, "xc")
         multiply(x_c, 384, 128)
 
         for acc, m, start, width in results:
             res = keep.tile([P, width], F32, name=f"res{start}_{m}", align_bytes=64)
-            if m == 0:
+            if (m == 0) != (start == 0):
                 nc.scalar.copy(res[:], acc[:])
             else:
                 nc.vector.tensor_copy(res[:], acc[:])

from contextlib import ExitStack

import concourse.mybir as mybir

F32 = mybir.dt.float32
BF16 = mybir.dt.bfloat16
I32 = mybir.dt.int32
U32 = mybir.dt.uint32
U16 = mybir.dt.uint16
U8 = mybir.dt.uint8
FP8X4 = mybir.dt.float8_e4m3fn_x4
ALU = mybir.AluOpType

P, J = 128, 4
K, M, T, S = 512, 256, 1024, 512
FLOPS = 2 * 2 * K * M * S
MASK = -(1 << 20)


def tile_list_heads_hl_none_kernel(tc, xT, w, wgt, offs, out):
    nc = tc.nc
    with ExitStack() as ctx:
        keep = ctx.enter_context(tc.tile_pool(name="keep", bufs=1))
        psum = ctx.enter_context(tc.psum_pool(name="psum", bufs=1))

        w_raw = keep.tile([P, J, M], F32, name="w_raw", align_bytes=64)
        lists = keep.tile([P, S // 16], U16, name="lists")
        weights = [keep.tile([P, n], F32, name=f"weights{n}", align_bytes=64) for n in (384, 128)]
        w_view = w.rearrange("(p j) n -> p j n", j=J)
        nc.sync.dma_start(w_raw[:, 0:2, :], w_view[:, 0:2, :])
        nc.sync.dma_start(w_raw[:, 2:4, :], w_view[:, 2:4, :])
        nc.sync.dma_start(lists[:], offs)
        nc.sync.dma_start(weights[0][:], wgt[:, 0:384])
        x_view = xT.rearrange("(p j) t -> p j t", j=J)
        planes = []
        for j in range(J):
            plane = keep.tile([P, T], F32, name=f"plane{j}", align_bytes=64)
            nc.sync.dma_start(plane[:], x_view[:, j, :])
            planes.append(plane)
        nc.sync.dma_start(weights[1][:], wgt[:, 384:512])

        w_hi = keep.tile([P, J, M], I32, name="w_hi", align_bytes=64)
        w_bf = keep.tile([P, 2 * M, J], BF16, name="w_bf", align_bytes=64)
        for h in range(2):
            js = slice(2 * h, 2 * h + 2)
            nc.vector.tensor_scalar(w_hi[:, js, :], w_raw[:, js, :].bitcast(I32), MASK, None, ALU.bitwise_and)
        nc.scalar.copy(w_bf[:, 0:M, :], w_hi[:].bitcast(F32).rearrange("p j n -> p n j"))
        nc.vector.tensor_tensor(
            w_bf[:, M : 2 * M, :],
            w_raw[:].rearrange("p j n -> p n j"),
            w_hi[:].bitcast(F32).rearrange("p j n -> p n j"),
            ALU.subtract,
        )

        def quantize(src, width, name):
            codes = keep.tile([P, width], U32, name=f"{name}_codes", align_bytes=64)
            scales = keep.tile([P, width], U8, name=f"{name}_scales", align_bytes=64)
            nc.vector.quantize_mx(
                out=codes[:].bitcast(FP8X4), scales=scales[:], in_=src.rearrange("p n j -> p (n j)")
            )
            return codes, scales

        picked = keep.tile([P, J, 384], F32, name="picked", align_bytes=64)
        xg = [keep.tile([P, n, J], BF16, name=f"xg{n}", align_bytes=64) for n in (384, 128)]

        def gather(j, start, width):
            h, c = start // 384, start % 384
            nc.vector.tensor_tensor(
                picked[:, j, c : c + width],
                planes[j][:].indirect(lists[:, start // 16 : (start + width) // 16]),
                weights[h][:, c : c + width],
                ALU.mult,
            )

        def interleave(pair, start, width):
            h, c = start // 384, start % 384
            nc.scalar.copy(
                xg[h][:, c : c + width, 2 * pair : 2 * pair + 2],
                picked[:, 2 * pair : 2 * pair + 2, c : c + width].rearrange("p j n -> p n j"),
            )

        results = []

        def multiply(x, start, width):
            for m in range(2):
                acc = psum.tile([P, width], F32, name=f"acc{start}_{m}")
                codes, scales = w_q
                for side in range(2):
                    cols = slice(side * M + m * P, side * M + (m + 1) * P)
                    nc.tensor.matmul_mx(
                        out=acc[:],
                        lhsT=codes[:, cols].bitcast(FP8X4),
                        lhsT_scale=scales[:, cols],
                        rhs=x[0][:].bitcast(FP8X4),
                        rhs_scale=x[1][:],
                        start=side == 0,
                        stop=side == 1,
                    )
                results.append((acc, m, start, width))

        w_q = quantize(w_bf[:], 2 * M, "w")
        gather(0, 0, 384)
        gather(1, 0, 384)
        interleave(0, 0, 384)
        gather(2, 0, 384)
        gather(3, 0, 256)
        interleave(1, 0, 256)
        gather(3, 256, 128)
        interleave(1, 256, 128)
        gather(0, 384, 128)
        gather(1, 384, 128)
        x_a = quantize(xg[0][:, 0:256, :], 256, "xa")
        multiply(x_a, 0, 256)
        interleave(0, 384, 128)
        gather(2, 384, 128)
        gather(3, 384, 128)
        interleave(1, 384, 128)
        x_b = quantize(xg[0][:, 256:384, :], 128, "xb")
        multiply(x_b, 256, 128)
        x_c = quantize(xg[1][:], 128, "xc")
        multiply(x_c, 384, 128)

        for acc, m, start, width in results:
            res = keep.tile([P, width], F32, name=f"res{start}_{m}", align_bytes=64)
            if (m == 0) != (start == 0):
                nc.scalar.copy(res[:], acc[:])
            else:
                nc.vector.tensor_copy(res[:], acc[:])
            nc.sync.dma_start(out[m * P : (m + 1) * P, start : start + width], res[:])
